import numpy as np
import ml_dtypes


def mxq(x, axis, fmt="e4m3"):
    dtype, down = {"e4m3": (ml_dtypes.float8_e4m3fn, 7), "e5m2": (ml_dtypes.float8_e5m2, 14)}[fmt]
    v = np.moveaxis(np.asarray(x, np.float32).astype(ml_dtypes.bfloat16).astype(np.float64), axis, -1)
    blocks = v.reshape(v.shape[:-1] + (-1, 32))
    amax = np.abs(blocks).max(-1, keepdims=True)
    byte = np.maximum(np.where(amax > 0, np.frexp(amax)[1] - 1 + 127, 0) - down, 1)
    scale = np.exp2(byte - 127.0)
    codes = (blocks / scale).astype(np.float32).astype(dtype).astype(np.float64)
    return np.moveaxis((codes * scale).reshape(v.shape), -1, axis)


WIDE = False


def mx_kscale(k):
    if not WIDE:
        return np.ones(k)
    levels = np.array([10, -10, 5, -5, 0])
    if k % 512:
        return np.exp2(np.random.permutation(np.resize(levels, k // 32))).repeat(32)
    a = np.empty((k // 512, 16))
    for p in range(k // 512):
        a[p, :8] = np.random.permutation(np.resize(levels, 8))
        for g in range(8):
            far = levels[np.abs(levels - a[p, g]) >= 10]
            a[p, g + 8] = far[np.random.randint(len(far))]
    return np.exp2(a.ravel()).repeat(32)


def f64(x):
    return np.asarray(x).astype(np.float64)


def striped(idx):
    return np.tile(np.asarray(idx).reshape(-1, 16).T, (8, 1)).astype(np.uint16)


def unstriped(offs):
    return offs[:16].T.reshape(-1).astype(np.int64)


E2M1 = np.array([0.0, 0.5, 1.0, 1.5, 2.0, 3.0, 4.0, 6.0, -0.0, -0.5, -1.0, -1.5, -2.0, -3.0, -4.0, -6.0])


def pack_weight(w, fmt):
    k, n = w.shape
    w = f64(np.asarray(w, np.float32).astype(ml_dtypes.bfloat16)).reshape(k // 32, 32, n)
    amax = np.abs(w).max(1)
    if fmt == "e4m3":
        byte = np.frexp(amax)[1] - 1 + 127 - 7
    else:
        mant, ex = np.frexp(amax / 6.0)
        byte = np.where(mant > 0.5, ex, ex - 1) + 127
    byte = np.clip(np.where(amax > 0, byte, 1), 1, 254)
    scaled = (w * np.exp2(127.0 - byte)[:, None, :]).reshape(k, n).astype(np.float32)
    by_word = np.ascontiguousarray(scaled.reshape(k // 512, 128, 4, n).transpose(0, 1, 3, 2))
    if fmt == "e4m3":
        words = by_word.astype(ml_dtypes.float8_e4m3fn).view(np.uint8)
    else:
        c = by_word.astype(ml_dtypes.float4_e2m1fn).view(np.uint8) & 0xF
        words = (c[..., 0::2] | (c[..., 1::2] << 4)).reshape(k // 512, 128, 2 * n)
    return np.ascontiguousarray(words), np.ascontiguousarray(byte.astype(np.uint8).reshape(k // 512, 16, n))


def unpack_weight(words, scales, fmt):
    g, _, n = scales.shape
    words = np.ascontiguousarray(words).reshape(g, 128, n, -1)
    if fmt == "e4m3":
        vals = words.view(ml_dtypes.float8_e4m3fn).astype(np.float64)
    else:
        nib = np.empty((g, 128, n, 4), np.uint8)
        nib[..., 0::2] = words & 0xF
        nib[..., 1::2] = words >> 4
        vals = E2M1[nib]
    vals = vals * np.repeat(np.exp2(scales.astype(np.float64) - 127.0), 8, axis=1)[..., None]
    return vals.transpose(0, 1, 3, 2).reshape(g * 512, n)


D, T, I, Q, E, V, M = 512, 2048, 512, 256, 512, 32, 1024


def setup_inputs():
    n = np.random.standard_normal
    idx = np.random.permutation(T)[:I]
    idx2 = np.random.permutation(M)[:Q]
    idx4 = np.random.permutation(I)[:I]
    fd = mx_kscale(D)
    fi = mx_kscale(I)
    ti = np.ones(T)
    ti[idx] = fi
    keysp = pack_weight(n((D, T)) / fd[:, None], "e4m3")
    return {
        "query": (n((D, Q)) * 1.0 / np.sqrt(D) * fd[:, None]).astype(np.float32),
        "keys_words": keysp[0],
        "keys_scales": keysp[1],
        "lam": (np.random.uniform(0.3, 0.8, (1, Q))).astype(np.float32),
        "rival": (np.random.uniform(0.5, 2.0, (Q, 1))).astype(np.float32),
        "os": (np.random.uniform(4.0, 16.0, (1, I)) * fi).astype(np.float32),
        "vals": (n((E, T)) / ti).astype(np.float32),
        "member": (n((E, M))).astype(np.float32),
        "mgain": np.tile(np.random.uniform(0.5, 2.0, M), (128, 1)).astype(np.float32),
        "offs": striped(idx),
        "offs2": striped(idx2),
        "offs4": striped(idx4),
    }


def reference(query, keys_words, keys_scales, lam, rival, os, vals, member, mgain, offs, offs2, offs4):
    idx = unstriped(offs)
    idx2 = unstriped(offs2)
    idx4 = unstriped(offs4)
    keysu = unpack_weight(keys_words, keys_scales, "e4m3")
    keysidxg = keysu[:, idx]
    queryq = mxq(f64(query), 0, "e4m3")
    a0 = keysidxg.T @ queryq
    ag = a0.reshape(I, V, Q // V).max(axis=2)
    ar = np.repeat(ag, Q // V, axis=1)
    s0 = a0 - ar * f64(lam)
    s = s0.T
    p = np.exp(s)
    r = p / (p + p[:, idx4] * f64(rival))
    w = r / np.sum(r, axis=1, keepdims=True)
    wo1 = w * f64(os)
    wt1 = wo1.T
    vt1 = f64(vals)[:, idx].T
    vt1q = mxq(vt1, 0, "e4m3")
    wt1q = mxq(wt1, 0, "e4m3")
    o = vt1q.T @ wt1q
    y = o * f64(mgain)[:1][:, idx2] + f64(member)[:, idx2]
    return y

from contextlib import ExitStack

import concourse.mybir as mybir
from concourse.masks import make_identity

D, T, I, Q, E, M = 512, 2048, 512, 256, 512, 1024
P = 128
GROUP = 8
FLOPS = 2 * D * I * Q + 2 * I * E * Q

F32 = mybir.dt.float32
BF16 = mybir.dt.bfloat16
I32 = mybir.dt.int32
U32 = mybir.dt.uint32
U16 = mybir.dt.uint16
U8 = mybir.dt.uint8
FP8X4 = mybir.dt.float8_e4m3fn_x4
ALU = mybir.AluOpType
ACT = mybir.ActivationFunctionType
AX = mybir.AxisListType


def tile_attend_groupbest_overlinked_bymember_kernel(
    tc, query, keys_words, keys_scales, lam, rival, slot_factor, vals, member, mgain, offs, offs2, offs4, out
):
    nc = tc.nc
    with ExitStack() as ctx:
        sb = ctx.enter_context(tc.tile_pool(name="sb", bufs=1))
        ps2 = ctx.enter_context(tc.psum_pool(name="ps2", bufs=2))
        ps1 = ctx.enter_context(tc.psum_pool(name="ps1", bufs=1))

        def tile(name, shape, dtype, tag=None):
            return sb.tile(shape, dtype, name=name, tag=tag or name, align_bytes=64)

        def block(n):
            return slice(P * n, P * (n + 1))

        offs_sb = tile("offs_sb", [P, I // 16], U16)
        offs2_sb = tile("offs2_sb", [P, Q // 16], U16)
        offs4_sb = tile("offs4_sb", [P, I // 16], U16)
        kw_pool = tile("kw_pool", [P, T], I32)
        ks_pool = tile("ks_pool", [P, T], U8)
        q_raw = [tile("q_raw%d" % h, [P, 4, P], F32) for h in range(2)]
        lam_c = tile("lam_c", [P, 2], F32)
        riv_c = tile("riv_c", [P, 2], F32)
        os_c = tile("os_c", [P, 4], F32)
        gain_pool = tile("gain_pool", [P, M], F32)
        v_pool = [tile("v_pool%d" % b, [P, T], F32) for b in range(4)]
        m_pool = [tile("m_pool%d" % b, [P, M], F32) for b in range(4)]
        ident = tile("ident", [P, P], F32)

        nc.gpsimd.memset(ks_pool[:].bitcast(I32), 0)
        make_identity(nc, ident[:])
        nc.vector.memset(gain_pool[:], 0.0)

        for g in range(4):
            nc.scalar.dma_start(
                ks_pool[32 * g : 32 * g + 4, :].bitcast(I32), keys_scales[0, 4 * g : 4 * g + 4, :].bitcast(I32)
            )
        nc.scalar.dma_start(gain_pool[0:1, :], mgain[0:1, :])
        nc.sync.dma_start(offs_sb[:], offs)
        nc.sync.dma_start(kw_pool[:], keys_words[0].rearrange("p n t -> p (n t)").bitcast(I32))
        nc.sync.dma_start(offs2_sb[:], offs2)
        for h in range(2):
            nc.sync.dma_start(q_raw[h][:], query.rearrange("(p j) q -> p j q", j=4)[:, :, block(h)])
        with nc.allow_non_contiguous_dma(reason="one value a partition"):
            nc.sync.dma_start(lam_c[:], lam.rearrange("o (h p) -> p (o h)", p=P))
        nc.sync.dma_start(m_pool[0][:], member[block(0), :])
        nc.sync.dma_start(v_pool[0][:], vals[block(0), :])
        nc.sync.dma_start(offs4_sb[:], offs4)
        with nc.allow_non_contiguous_dma(reason="one value a partition"):
            nc.sync.dma_start(riv_c[:], rival.rearrange("(h p) o -> p (h o)", p=P))
        nc.sync.dma_start(os_c[:], slot_factor.rearrange("o (p c) -> (o p) c", c=4))
        for b in range(1, 4):
            nc.sync.dma_start(v_pool[b][:], vals[block(b), :])
        for b in range(1, 4):
            nc.sync.dma_start(m_pool[b][:], member[block(b), :])

        ks = tile("ks", [P, I], U8)
        kw = tile("kw", [P, I], U32)
        q_bf = [tile("q_bf%d" % h, [P, P, 4], BF16) for h in range(2)]
        q_codes = tile("q_codes", [P, Q], U32)
        q_scales = tile("q_scales", [P, Q], U8)
        nc.vector.tensor_copy(ks[:], ks_pool[:].indirect(offs_sb[:]))
        for k in range(2):
            nc.vector.tensor_copy(
                kw[:, 256 * k : 256 * (k + 1)], kw_pool[:].bitcast(U32).indirect(offs_sb[:, 16 * k : 16 * (k + 1)])
            )
        for h in range(2):
            nc.scalar.copy(
                q_bf[h][:].rearrange("p (c i) t -> p c t i", i=4),
                q_raw[h][:].rearrange("p t (c i) -> p c t i", i=4),
            )
            nc.vector.quantize_mx(
                q_codes[:, block(h)].bitcast(FP8X4), q_scales[:, block(h)], q_bf[h][:].rearrange("p q t -> p (q t)")
            )

        a0 = [ps2.tile([P, 512], F32, name="acc") for h in range(2)]
        for h in range(2):
            for c in range(4):
                nc.tensor.matmul_mx(
                    a0[h][:, block(c)], lhsT=kw[:, block(c)].bitcast(FP8X4), lhsT_scale=ks[:, block(c)],
                    rhs=q_codes[:, block(h)].bitcast(FP8X4), rhs_scale=q_scales[:, block(h)], start=True, stop=True,
                )
        lam_ps = ps1.tile([P, 512], F32, name="lam_ps")
        for h in range(2):
            nc.tensor.transpose(lam_ps[:, block(h)], lam_c[:, h : h + 1].to_broadcast([P, P]), ident[:])

        gain_g = tile("gain_g", [P, Q], F32)
        nc.scalar.activation(gain_g[:], gain_pool[:].indirect(offs2_sb[:]), ACT.Copy)
        gcols_ps = ps2.tile([P, 512], F32, name="turn")
        for h in range(2):
            nc.tensor.transpose(gcols_ps[:, block(h)], gain_g[:, block(h)], ident[:])
        gcols = tile("gcols", [P, 2], F32)
        nc.scalar.copy(gcols[:], gcols_ps[:, 0:Q:P])
        gain_ps = ps2.tile([P, 512], F32, name="turn")
        for h in range(2):
            nc.tensor.transpose(gain_ps[:, block(h)], gcols[:, h : h + 1].to_broadcast([P, P]), ident[:])
        gain = tile("gain", [P, Q], F32)
        nc.scalar.copy(gain[:], gain_ps[:, 0:Q])

        a_sb = [tile("a_sb%d" % h, [P, 512], F32) for h in range(2)]
        u_sb = [tile("u_sb%d" % h, [P, 512], F32) for h in range(2)]
        nc.scalar.copy(a_sb[1][:], a0[1][:])
        for h in range(2):
            negbest = tile("negbest%d" % h, [P, 64], F32, "negbest")
            nc.vector.tensor_reduce(
                negbest[:], a0[h][:].rearrange("p (g j) -> p g j", j=GROUP), AX.X, ALU.max, negate=True
            )
            if h == 0:
                nc.scalar.copy(a_sb[0][:], a0[0][:])
            nc.vector.tensor_tensor(
                u_sb[h][:].rearrange("p (c v j) -> p c v j", c=4, j=GROUP),
                negbest[:].rearrange("p (c v) -> p c v", c=4).unsqueeze(3).broadcast_to([P, 4, 16, GROUP]),
                lam_ps[:, block(h)].rearrange("p (v j) -> p v j", j=GROUP).unsqueeze(1).broadcast_to([P, 4, 16, GROUP]),
                ALU.mult,
            )
        s_ps = [ps2.tile([P, 512], F32, name="sc") for h in range(2)]
        for h in range(2):
            for k, src in enumerate((a_sb[h], u_sb[h])):
                for c in range(4):
                    nc.tensor.matmul(
                        s_ps[h][:, block(c)], src[:, block(c)], ident[:], is_transpose=True,
                        start=(k == 0 and c == 0), stop=(k == 1 and c == 3),
                    )

        m_g = {}

        def gather_member(b, tag):
            m_g[b] = tile("m_g%d" % b, [P, Q], F32, tag)
            nc.scalar.activation(m_g[b][:], m_pool[b][:].indirect(offs2_sb[:]), ACT.Copy)

        def turn_words(src, bank, first):
            words = src[:].bitcast(F32)
            for u in range(2):
                nc.tensor.transpose(bank[:, block(first + u)], words[:, u : 2 * P : 2], ident[:])

        def weave_words(dst, bank, n):
            nc.scalar.copy(
                dst[:].rearrange("p e t -> p (e t)").bitcast(F32).rearrange("p (k e u) -> p k e u", k=n, u=2),
                bank[:, 0 : 2 * P * n].rearrange("p (k u e) -> p k e u", k=n, u=2),
            )

        def gather_vals(b, on_scalar, tag, bank):
            v_g = tile("v_g%d" % b, [P, I], BF16, tag)
            if on_scalar:
                nc.scalar.activation(v_g[:], v_pool[b][:].indirect(offs_sb[:]), ACT.Copy)
            else:
                nc.vector.tensor_copy(v_g[:], v_pool[b][:].indirect(offs_sb[:]))
            turn_words(v_g, bank, 2 * (b % 2))

        def quantise(codes, scales, src):
            nc.vector.quantize_mx(codes.bitcast(FP8X4), scales, src[:].rearrange("p e t -> p (e t)"))

        gather_member(0, "q_codes")
        p_sb = [tile("p_sb%d" % h, [P, I], F32) for h in range(2)]
        ip_sb = [tile("ip_sb%d" % h, [P, I], F32) for h in range(2)]
        for h in range(2):
            nc.scalar.activation(p_sb[h][:], s_ps[h][:], ACT.Exp)
            nc.scalar.activation(ip_sb[h][:], s_ps[h][:], ACT.Exp, scale=-1.0)
        vt_ps = [ps2.tile([P, 512], F32, name="turn") for pair in range(2)]
        gather_vals(0, False, "negbest", vt_ps[0])
        os_ps = ps1.tile([P, 512], F32, name="os_ps")
        for c in range(4):
            nc.tensor.transpose(os_ps[:, block(c)], os_c[:, c : c + 1].to_broadcast([P, P]), ident[:])
        x_sb = [tile("x_sb0", [P, I], F32, "v_pool0"), tile("x_sb1", [P, I], F32)]
        for h in range(2):
            for k in range(2):
                cs = slice(256 * k, 256 * (k + 1))
                nc.vector.tensor_tensor(
                    x_sb[h][:, cs], p_sb[h][:].indirect(offs4_sb[:, 16 * k : 16 * (k + 1)]), ip_sb[h][:, cs], ALU.mult
                )
        gather_vals(1, False, "ip_sb1", vt_ps[0])
        y_sb = [tile("y_sb%d" % h, [P, I], F32) for h in range(2)]
        r_sb = [tile("r_sb0", [P, I], F32, "v_pool1"), tile("r_sb1", [P, I], F32)]
        rsum = [tile("rsum%d" % h, [P, 1], F32) for h in range(2)]
        rinv = [tile("rinv%d" % h, [P, 1], F32) for h in range(2)]
        for h in range(2):
            nc.scalar.activation(y_sb[h][:], x_sb[h][:], ACT.Abs_reciprocal_sqrt, bias=1.0, scale=riv_c[:, h : h + 1])
        nc.vector.scalar_tensor_tensor(r_sb[0][:], y_sb[0][:], 1.0, y_sb[0][:], ALU.mult, ALU.mult, accum_out=rsum[0][:])
        nc.scalar.activation(r_sb[1][:], y_sb[1][:], ACT.Square, accum_out=rsum[1][:])
        vt_bf = [tile("vt_bf%d" % pair, [P, 2 * P, 4], BF16) for pair in range(2)]
        weave_words(vt_bf[0], vt_ps[0], 2)
        gather_vals(2, True, "y_sb1", vt_ps[1])
        w_bf = [tile("w_bf%d" % h, [P, I], BF16) for h in range(2)]
        wt_bf = [tile("wt_bf0", [P, P, 4], BF16, "v_pool2"), tile("wt_bf1", [P, P, 4], BF16)]
        for h in range(2):
            nc.vector.reciprocal(rinv[h][:], rsum[h][:])
        for h in range(2):
            nc.vector.scalar_tensor_tensor(
                w_bf[h][:].rearrange("p (n c) -> p n c", c=4), r_sb[h][:].rearrange("p (n c) -> p n c", c=4),
                rinv[h][:], os_ps[:].rearrange("p (c n) -> p n c", c=4), ALU.mult, ALU.mult,
            )
            wt_ps = ps2.tile([P, 512], F32, name="sc")
            turn_words(w_bf[h], wt_ps, 0)
            weave_words(wt_bf[h], wt_ps, 1)
        gather_vals(3, False, "r_sb1", vt_ps[1])
        v_codes = [tile("v_codes0", [P, 2 * P], U32, "v_pool3"), tile("v_codes1", [P, 2 * P], U32)]
        v_scales = [tile("v_scales%d" % pair, [P, 2 * P], U8) for pair in range(2)]
        quantise(v_codes[0][:], v_scales[0][:], vt_bf[0])
        w_codes = tile("w_codes", [P, Q], U32, "vt_bf0")
        w_scales = tile("w_scales", [P, Q], U8)
        for h in range(2):
            quantise(w_codes[:, block(h)], w_scales[:, block(h)], wt_bf[h])
        weave_words(vt_bf[1], vt_ps[1], 2)
        quantise(v_codes[1][:], v_scales[1][:], vt_bf[1])
        gather_member(1, "w_bf1")
        gather_member(2, "r_sb1")
        gather_member(3, None)

        og = [tile("og%d" % pair, [P, 2, Q], F32) for pair in range(2)]
        res = [tile("res%d" % b, [P, Q], F32) for b in range(4)]
        for pair in range(2):
            o_ps = ps2.tile([P, 512], F32, name="acc")
            for k in range(2):
                nc.tensor.matmul_mx(
                    o_ps[:, Q * k : Q * (k + 1)], lhsT=v_codes[pair][:, block(k)].bitcast(FP8X4),
                    lhsT_scale=v_scales[pair][:, block(k)],
                    rhs=w_codes[:].bitcast(FP8X4), rhs_scale=w_scales[:], start=True, stop=True,
                )
            nc.vector.tensor_tensor(
                og[pair][:], o_ps[:].rearrange("p (k q) -> p k q", k=2),
                gain[:].unsqueeze(1).broadcast_to([P, 2, Q]), ALU.mult,
            )
            for k in range(2):
                b = 2 * pair + k
                nc.vector.tensor_tensor(res[b][:], og[pair][:, k, :], m_g[b][:], ALU.add)
                nc.sync.dma_start(out[block(b), :], res[b][:])
